import numpy as np
import ml_dtypes


def mxq(x, axis, fmt="e4m3"):
    dtype, down = {"e4m3": (ml_dtypes.float8_e4m3fn, 7), "e5m2": (ml_dtypes.float8_e5m2, 14)}[fmt]
    v = np.moveaxis(np.asarray(x, np.float32).astype(ml_dtypes.bfloat16).astype(np.float64), axis, -1)
    blocks = v.reshape(v.shape[:-1] + (-1, 32))
    amax = np.abs(blocks).max(-1, keepdims=True)
    byte = np.maximum(np.where(amax > 0, np.frexp(amax)[1] - 1 + 127, 0) - down, 1)
    scale = np.exp2(byte - 127.0)
    codes = (blocks / scale).astype(np.float32).astype(dtype).astype(np.float64)
    return np.moveaxis((codes * scale).reshape(v.shape), -1, axis)


WIDE = False


def mx_kscale(k):
    if not WIDE:
        return np.ones(k)
    levels = np.array([10, -10, 5, -5, 0])
    if k % 512:
        return np.exp2(np.random.permutation(np.resize(levels, k // 32))).repeat(32)
    a = np.empty((k // 512, 16))
    for p in range(k // 512):
        a[p, :8] = np.random.permutation(np.resize(levels, 8))
        for g in range(8):
            far = levels[np.abs(levels - a[p, g]) >= 10]
            a[p, g + 8] = far[np.random.randint(len(far))]
    return np.exp2(a.ravel()).repeat(32)


def f64(x):
    return np.asarray(x).astype(np.float64)


def striped(idx):
    return np.tile(idx.reshape(-1, 16).T, (8, 1)).astype(np.uint16)


def unstriped(offs):
    return offs[:16].T.reshape(-1).astype(np.int64)


def striped8(idx):
    return np.concatenate([x.reshape(-1, 16).T for x in idx]).astype(np.uint16)


def runs(offs, k):
    lists = np.stack([offs[16 * r : 16 * r + 16].T.reshape(-1) for r in range(8)]).astype(np.int64)
    return lists[np.arange(k) % 512 // 64]


def pack_weight(w):
    k, n = w.shape
    w = f64(np.asarray(w, np.float32).astype(ml_dtypes.bfloat16)).reshape(k // 32, 32, n)
    amax = np.abs(w).max(1)
    byte = np.clip(np.where(amax > 0, np.frexp(amax)[1] - 1 + 127 - 7, 1), 1, 254)
    scaled = (w * np.exp2(127.0 - byte)[:, None, :]).reshape(k, n).astype(np.float32)
    words = np.ascontiguousarray(scaled.reshape(k // 512, 128, 4, n).transpose(0, 1, 3, 2)).astype(ml_dtypes.float8_e4m3fn).view(np.uint8)
    return words, np.ascontiguousarray(byte.astype(np.uint8).reshape(k // 512, 16, n))


def unpack_weight(words, scales):
    g, p, n, _ = words.shape
    vals = np.ascontiguousarray(words).view(ml_dtypes.float8_e4m3fn).astype(np.float64) * np.repeat(np.exp2(scales.astype(np.float64) - 127.0), 8, axis=1)[..., None]
    return vals.transpose(0, 1, 3, 2).reshape(g * 512, n)

def planes(y):
    n, m = y.shape
    v = y.astype(np.float32).astype(ml_dtypes.bfloat16).astype(np.float64).reshape(n // 32, 32, m)
    top = np.abs(v).max(1)
    byte = np.clip(np.where(top > 0, np.frexp(top)[1] - 1 + 127 - 7, 1), 1, 254)
    codes = (v * np.exp2(127.0 - byte)[:, None, :]).reshape(n, m).astype(np.float32).astype(ml_dtypes.float8_e4m3fn).view(np.uint8)
    words = codes.reshape(n // 512, 128, 4, m).transpose(0, 1, 3, 2)
    return np.ascontiguousarray(words), np.ascontiguousarray(byte.astype(np.uint8).reshape(n // 512, 16, m))


K, T, S, V, N, H = 512, 2048, 512, 256, 512, 512


def setup_inputs():
    n = np.random.standard_normal
    s = mx_kscale(K)[:, None]
    u = mx_kscale(H)
    packed_xT = pack_weight(n((K, T)) * s)
    packed_w1 = pack_weight(n((K, H)) / np.sqrt(K) / s)
    packed_w2 = pack_weight(n((H, N)) / np.sqrt(H) / u[:, None])
    perm = np.stack([np.random.permutation(S) for _ in range(8)])
    perm2 = np.stack([np.random.permutation(S) for _ in range(8)])
    return {
        "x_words": packed_xT[0],
        "x_scales": packed_xT[1],
        "w1_words": packed_w1[0],
        "w1_scales": packed_w1[1],
        "gn": (np.random.uniform(0.5, 1.5, (H, 1)) * u[:, None]).astype(np.float32),
        "w2_words": packed_w2[0],
        "w2_scales": packed_w2[1],
        "offs": striped(np.random.permutation(T)[:S]),
        "la": striped8(perm[:, :V]),
        "lb": striped8(perm[:, V:]),
        "ma": striped8(perm2[:, :V]),
        "mb": striped8(perm2[:, V:]),
    }


def reference(x_words, x_scales, w1_words, w1_scales, gn, w2_words, w2_scales, offs, la, lb, ma, mb):
    xq = unpack_weight(x_words, x_scales)[:, unstriped(offs)]
    y = unpack_weight(w1_words, w1_scales).T @ xq
    m1 = 0.5 * (y[np.arange(H)[:, None], runs(la, H)] + y[np.arange(H)[:, None], runs(lb, H)])
    m0 = y[np.arange(H)[:, None], runs(lb, H)] - (0.5 * m1)
    h0 = np.zeros((H, S))
    h0[np.arange(H)[:, None], runs(lb, H)] = m0
    h = h0.copy()
    h[np.arange(H)[:, None], runs(la, H)] = m1
    m3 = np.minimum(h[np.arange(H)[:, None], runs(ma, H)], h[np.arange(H)[:, None], runs(mb, H)])
    m2 = np.maximum(h[np.arange(H)[:, None], runs(ma, H)], h[np.arange(H)[:, None], runs(mb, H)])
    h2 = np.zeros((H, S))
    h2[np.arange(H)[:, None], runs(ma, H)] = m2
    h3 = h2.copy()
    h3[np.arange(H)[:, None], runs(mb, H)] = m3
    z = f64(gn) * h3
    out_0 = unpack_weight(w2_words, w2_scales).T @ mxq(z, 0, "e4m3")
    return (out_0,) + planes(out_0)

@@ -1,0 +1,163 @@
+from contextlib import ExitStack
+
+import concourse.mybir as mybir
+
+F32 = mybir.dt.float32
+BF16 = mybir.dt.bfloat16
+I32 = mybir.dt.int32
+U32 = mybir.dt.uint32
+U16 = mybir.dt.uint16
+U8 = mybir.dt.uint8
+FP8X4 = mybir.dt.float8_e4m3fn_x4
+ALU = mybir.AluOpType
+COPY = mybir.ActivationFunctionType.Copy
+
+P = 128
+PACK = 4
+T, S, V = 2048, 512, 256
+CHUNK = 128
+FLOPS = 2 * 2 * 512 * 512 * 512
+
+
+def load_scale_rows(queue, plane, rows):
+    rows32 = rows.bitcast(I32)
+    plane32 = plane[:].bitcast(I32)
+    for q in range(4):
+        queue.dma_start(out=plane32[32 * q : 32 * q + 4, :], in_=rows32[4 * q : 4 * q + 4, :])
+
+
+def words_view(words):
+    return words[0].rearrange("p n t -> p (n t)").bitcast(I32)
+
+
+def tile_picked_gossip2_none_po_kernel(
+    tc, x_words, x_scales, w1_words, w1_scales, gn, w2_words, w2_scales, offs, la, lb, ma, mb, out_0, out_1, out_2
+):
+    nc = tc.nc
+    with ExitStack() as ctx:
+        keep = ctx.enter_context(tc.tile_pool(name="keep", bufs=1))
+        psum = ctx.enter_context(tc.psum_pool(name="psum", bufs=1))
+
+        def tiles(name, shape, dtype, count=PACK):
+            return [keep.tile(shape, dtype, name="%s%d" % (name, i), align_bytes=64) for i in range(count)]
+
+        offs_sb = keep.tile([P, S // 16], U16, name="offs_sb")
+        la_sb = keep.tile([P, V // 16], U16, name="la_sb")
+        lb_sb = keep.tile([P, V // 16], U16, name="lb_sb")
+        ma_sb = keep.tile([P, V // 16], U16, name="ma_sb")
+        mb_sb = keep.tile([P, V // 16], U16, name="mb_sb")
+        xw = keep.tile([P, T], U32, name="xw", align_bytes=64)
+        xs = keep.tile([P, T], U8, name="xs", align_bytes=64)
+        w1w = keep.tile([P, 512], U32, name="w1w", align_bytes=64)
+        w1s = keep.tile([P, 512], U8, name="w1s", align_bytes=64)
+        w2w = keep.tile([P, 512], U32, name="w2w", align_bytes=64)
+        w2s = keep.tile([P, 512], U8, name="w2s", align_bytes=64)
+        gn_sb = keep.tile([P, PACK], F32, name="gn_sb")
+        h3 = tiles("h3_", [P, S], F32)
+
+        nc.vector.memset(xs[:].bitcast(I32), 0)
+        nc.vector.memset(w1s[:].bitcast(I32), 0)
+        nc.vector.memset(w2s[:].bitcast(I32), 0)
+        nc.sync.dma_start(offs_sb[:], offs)
+        nc.scalar.dma_start(out=w1w[:].bitcast(I32), in_=words_view(w1_words))
+        load_scale_rows(nc.sync, xs, x_scales[0])
+        nc.sync.dma_start(out=xw[:].bitcast(I32), in_=words_view(x_words))
+        load_scale_rows(nc.scalar, w1s, w1_scales[0])
+        nc.sync.dma_start(la_sb[:], la)
+        nc.sync.dma_start(lb_sb[:], lb)
+        nc.sync.dma_start(out=w2w[:].bitcast(I32), in_=words_view(w2_words))
+        load_scale_rows(nc.sync, w2s, w2_scales[0])
+        nc.sync.dma_start(ma_sb[:], ma)
+        nc.sync.dma_start(mb_sb[:], mb)
+        nc.sync.dma_start(out=gn_sb[:], in_=gn.rearrange("(p t) o -> p (t o)", t=PACK))
+        for t in range(PACK):
+            nc.vector.memset(h3[t][:], 0.0)
+
+        def deal(name, words, scales):
+            dw = keep.tile([P, PACK, P], U32, name=name + "dw", align_bytes=64)
+            ds = keep.tile([P, PACK, P], U8, name=name + "ds", align_bytes=64)
+            nc.vector.tensor_copy(out=dw[:].bitcast(I32), in_=words[:].bitcast(I32).rearrange("p (m t) -> p t m", t=PACK))
+            nc.vector.tensor_copy(out=ds[:], in_=scales[:].rearrange("p (m t) -> p t m", t=PACK))
+            return dw, ds
+
+        w1dw, w1ds = deal("w1", w1w, w1s)
+        xqw = keep.tile([P, S], U32, name="xqw", align_bytes=64)
+        xqs = keep.tile([P, S], U8, name="xqs", align_bytes=64)
+        nc.vector.tensor_copy(xqs[:], xs[:].indirect(offs_sb[:]))
+        halves = [slice(0, S // 2), slice(S // 2, S)]
+        for u, cols in enumerate(halves):
+            nc.vector.tensor_copy(xqw[:, cols], xw[:].indirect(offs_sb[:, 16 * u : 16 * (u + 1)]))
+        w2dw, w2ds = deal("w2", w2w, w2s)
+
+        yh = tiles("yh", [P, S], F32)
+        pieces = [(0, cols) for cols in halves] + [(t, slice(0, S)) for t in range(1, PACK)]
+        for i, (t, cols) in enumerate(pieces):
+            acc = psum.tile([P, cols.stop - cols.start], F32, name="bank%d" % i)
+            nc.tensor.matmul_mx(
+                out=acc[:], lhsT=w1dw[:, t, :].bitcast(FP8X4), lhsT_scale=w1ds[:, t, :],
+                rhs=xqw[:, cols].bitcast(FP8X4), rhs_scale=xqs[:, cols], start=True, stop=True,
+            )
+            nc.scalar.activation(yh[t][:, cols], acc[:], COPY, scale=0.5)
+
+        ah = tiles("ah", [P, V], F32)
+        bh = tiles("bh", [P, V], F32)
+        pa = tiles("pa", [P, V], F32)
+        pb = tiles("pb", [P, V], F32)
+        h = tiles("h", [P, S], F32)
+        for t in range(PACK):
+            nc.vector.tensor_copy(ah[t][:], yh[t][:].indirect(la_sb[:]))
+            nc.vector.tensor_copy(bh[t][:], yh[t][:].indirect(lb_sb[:]))
+            nc.scalar.activation(pa[t][:], ah[t][:], COPY, scale=-0.5)
+            nc.scalar.activation(pb[t][:], bh[t][:], COPY, scale=1.5)
+        for t in range(PACK):
+            nc.vector.tensor_tensor(h[t][:].indirect(la_sb[:]), ah[t][:], bh[t][:], ALU.add)
+        for t in range(PACK):
+            nc.vector.tensor_tensor(h[t][:].indirect(lb_sb[:]), pa[t][:], pb[t][:], ALU.add)
+
+        ca = tiles("ca", [P, V], F32)
+        cb = tiles("cb", [P, V], F32)
+        hi = tiles("hi", [P, V], F32)
+        lo = tiles("lo", [P, V], F32)
+        for t in range(PACK):
+            nc.vector.tensor_copy(ca[t][:], h[t][:].indirect(ma_sb[:]))
+            nc.vector.tensor_copy(cb[t][:], h[t][:].indirect(mb_sb[:]))
+        for t in range(PACK):
+            nc.vector.tensor_tensor(hi[t][:], ca[t][:], cb[t][:], ALU.max)
+            nc.vector.tensor_tensor(lo[t][:], ca[t][:], cb[t][:], ALU.min)
+        z = keep.tile([P, S, PACK], BF16, name="z", align_bytes=64)
+        for t in range(PACK):
+            nc.vector.tensor_copy(h3[t][:].indirect(ma_sb[:]), hi[t][:])
+        for t in range(PACK):
+            nc.vector.tensor_copy(h3[t][:].indirect(mb_sb[:]), lo[t][:])
+            if t < PACK - 1:
+                nc.scalar.activation(z[:, :, t], h3[t][:], COPY, scale=gn_sb[:, t : t + 1])
+
+        last = PACK - 1
+        zw = keep.tile([P, S], U32, name="zw", align_bytes=64)
+        zs = keep.tile([P, S], U8, name="zs", align_bytes=64)
+        o32 = keep.tile([P, PACK, S], F32, name="o32", align_bytes=64)
+        o16 = keep.tile([P, S, PACK], BF16, name="o16", align_bytes=64)
+        ow = keep.tile([P, S], U32, name="ow", align_bytes=64)
+        osc = keep.tile([P, S], U8, name="osc", align_bytes=64)
+        out_rows = out_0.rearrange("(p t) n -> p t n", t=PACK)
+        chunks = [slice(c, c + CHUNK) for c in range(0, S, CHUNK)]
+        for c, cols in enumerate(chunks):
+            nc.scalar.activation(z[:, cols, last], h3[last][:, cols], COPY, scale=gn_sb[:, last : last + 1])
+        for c, cols in enumerate(chunks):
+            nc.vector.quantize_mx(out=zw[:, cols].bitcast(FP8X4), scales=zs[:, cols], in_=z[:, cols, :].rearrange("p n t -> p (n t)"))
+            acc = psum.tile([P, PACK, CHUNK], F32, name="bank%d" % (c + 1))
+            for t in range(PACK):
+                nc.tensor.matmul_mx(
+                    out=acc[:, t, :], lhsT=w2dw[:, t, :].bitcast(FP8X4), lhsT_scale=w2ds[:, t, :],
+                    rhs=zw[:, cols].bitcast(FP8X4), rhs_scale=zs[:, cols], start=True, stop=True,
+                )
+            nc.scalar.copy(o32[:, :, cols], acc[:])
+            nc.sync.dma_start(out=out_rows[:, :, cols], in_=o32[:, :, cols])
+        for c, cols in enumerate(chunks):
+            nc.vector.tensor_copy(o16[:, cols, :], o32[:, :, cols].rearrange("p t n -> p n t"))
+            nc.vector.quantize_mx(out=ow[:, cols].bitcast(FP8X4), scales=osc[:, cols], in_=o16[:, cols, :].rearrange("p n t -> p (n t)"))
+        nc.sync.dma_start(out=words_view(out_1), in_=ow[:].bitcast(I32))
+        rows32 = out_2[0].bitcast(I32)
+        for q in range(4):
+            queue = nc.scalar if q % 2 else nc.sync
+            queue.dma_start(out=rows32[4 * q : 4 * q + 4, :], in_=osc[:].bitcast(I32)[32 * q : 32 * q + 4, :])

@@ -30,64 +30,64 @@ def words_view(words):
     return words[0].rearrange("p n t -> p (n t)").bitcast(I32)
 
 
+def deal(nc, dealt, raw, planes):
+    nc.vector.tensor_copy(
+        out=dealt.rearrange("p t m -> p m t")[:, :, planes], in_=raw.rearrange("p (m t) -> p m t", t=PACK)[:, :, planes]
+    )
+
+
 def tile_picked_gossip2_none_po_kernel(
     tc, x_words, x_scales, w1_words, w1_scales, gn, w2_words, w2_scales, offs, la, lb, ma, mb, out_0, out_1, out_2
 ):
     nc = tc.nc
     with ExitStack() as ctx:
         keep = ctx.enter_context(tc.tile_pool(name="keep", bufs=1))
+        late = ctx.enter_context(tc.tile_pool(name="late", bufs=1))
         psum = ctx.enter_context(tc.psum_pool(name="psum", bufs=1))
 
         def tiles(name, shape, dtype, count=PACK):
             return [keep.tile(shape, dtype, name="%s%d" % (name, i), align_bytes=64) for i in range(count)]
 
+        every = slice(0, PACK)
+        last = PACK - 1
         offs_sb = keep.tile([P, S // 16], U16, name="offs_sb")
         la_sb = keep.tile([P, V // 16], U16, name="la_sb")
         lb_sb = keep.tile([P, V // 16], U16, name="lb_sb")
         ma_sb = keep.tile([P, V // 16], U16, name="ma_sb")
         mb_sb = keep.tile([P, V // 16], U16, name="mb_sb")
         xw = keep.tile([P, T], U32, name="xw", align_bytes=64)
-        xs = keep.tile([P, T], U8, name="xs", align_bytes=64)
-        w1w = keep.tile([P, 512], U32, name="w1w", align_bytes=64)
-        w1s = keep.tile([P, 512], U8, name="w1s", align_bytes=64)
-        w2w = keep.tile([P, 512], U32, name="w2w", align_bytes=64)
-        w2s = keep.tile([P, 512], U8, name="w2s", align_bytes=64)
-        gn_sb = keep.tile([P, PACK], F32, name="gn_sb")
-        h3 = tiles("h3_", [P, S], F32)
+        xs = keep.tile([P, T], U8, name="xs", tag="xs", align_bytes=64)
+        ww = keep.tile([P, 512], U32, name="ww", align_bytes=64)
+        ws = keep.tile([P, 512], U8, name="ws", align_bytes=64)
 
         nc.vector.memset(xs[:].bitcast(I32), 0)
-        nc.vector.memset(w1s[:].bitcast(I32), 0)
-        nc.vector.memset(w2s[:].bitcast(I32), 0)
+        nc.gpsimd.memset(ws[:].bitcast(I32), 0)
         nc.sync.dma_start(offs_sb[:], offs)
-        nc.scalar.dma_start(out=w1w[:].bitcast(I32), in_=words_view(w1_words))
-        load_scale_rows(nc.sync, xs, x_scales[0])
-        nc.sync.dma_start(out=xw[:].bitcast(I32), in_=words_view(x_words))
-        load_scale_rows(nc.scalar, w1s, w1_scales[0])
         nc.sync.dma_start(la_sb[:], la)
         nc.sync.dma_start(lb_sb[:], lb)
-        nc.sync.dma_start(out=w2w[:].bitcast(I32), in_=words_view(w2_words))
-        load_scale_rows(nc.sync, w2s, w2_scales[0])
+        nc.sync.dma_start(out=ww[:].bitcast(I32), in_=words_view(w1_words))
+        nc.sync.dma_start(out=xw[:].bitcast(I32), in_=words_view(x_words))
+        load_scale_rows(nc.scalar, xs, x_scales[0])
+        load_scale_rows(nc.gpsimd, ws, w1_scales[0])
         nc.sync.dma_start(ma_sb[:], ma)
         nc.sync.dma_start(mb_sb[:], mb)
-        nc.sync.dma_start(out=gn_sb[:], in_=gn.rearrange("(p t) o -> p (t o)", t=PACK))
-        for t in range(PACK):
-            nc.vector.memset(h3[t][:], 0.0)
 
-        def deal(name, words, scales):
-            dw = keep.tile([P, PACK, P], U32, name=name + "dw", align_bytes=64)
-            ds = keep.tile([P, PACK, P], U8, name=name + "ds", align_bytes=64)
-            nc.vector.tensor_copy(out=dw[:].bitcast(I32), in_=words[:].bitcast(I32).rearrange("p (m t) -> p t m", t=PACK))
-            nc.vector.tensor_copy(out=ds[:], in_=scales[:].rearrange("p (m t) -> p t m", t=PACK))
-            return dw, ds
-
-        w1dw, w1ds = deal("w1", w1w, w1s)
+        w1dw = keep.tile([P, PACK, P], U32, name="w1dw", align_bytes=64)
+        w1ds = keep.tile([P, PACK, P], U8, name="w1ds", align_bytes=64)
+        deal(nc, w1dw[:].bitcast(I32), ww[:].bitcast(I32), every)
         xqw = keep.tile([P, S], U32, name="xqw", align_bytes=64)
         xqs = keep.tile([P, S], U8, name="xqs", align_bytes=64)
         nc.vector.tensor_copy(xqs[:], xs[:].indirect(offs_sb[:]))
+        deal(nc, w1ds[:], ws[:], slice(0, 1))
         halves = [slice(0, S // 2), slice(S // 2, S)]
         for u, cols in enumerate(halves):
             nc.vector.tensor_copy(xqw[:, cols], xw[:].indirect(offs_sb[:, 16 * u : 16 * (u + 1)]))
-        w2dw, w2ds = deal("w2", w2w, w2s)
+        deal(nc, w1ds[:], ws[:], slice(1, PACK))
+
+        gn_sb = keep.tile([P, PACK], F32, name="gn_sb", tag="xs", align_bytes=64)
+        nc.sync.dma_start(out=gn_sb[:], in_=gn.rearrange("(p t) o -> p (t o)", t=PACK))
+        nc.sync.dma_start(out=ww[:].bitcast(I32), in_=words_view(w2_words))
+        load_scale_rows(nc.sync, ws, w2_scales[0])
 
         yh = tiles("yh", [P, S], F32)
         pieces = [(0, cols) for cols in halves] + [(t, slice(0, S)) for t in range(1, PACK)]
@@ -117,7 +117,8 @@ def tile_picked_gossip2_none_po_kernel(
         ca = tiles("ca", [P, V], F32)
         cb = tiles("cb", [P, V], F32)
         hi = tiles("hi", [P, V], F32)
-        lo = tiles("lo", [P, V], F32)
+        lo = tiles("lo", [P, V], F32, last) + [late.tile([P, V], F32, name="lo_last", offset=1536)]
+        h3 = tiles("h3_", [P, S], F32)
         for t in range(PACK):
             nc.vector.tensor_copy(ca[t][:], h[t][:].indirect(ma_sb[:]))
             nc.vector.tensor_copy(cb[t][:], h[t][:].indirect(mb_sb[:]))
@@ -129,10 +130,14 @@ def tile_picked_gossip2_none_po_kernel(
             nc.vector.tensor_copy(h3[t][:].indirect(ma_sb[:]), hi[t][:])
         for t in range(PACK):
             nc.vector.tensor_copy(h3[t][:].indirect(mb_sb[:]), lo[t][:])
-            if t < PACK - 1:
+            if t < last:
                 nc.scalar.activation(z[:, :, t], h3[t][:], COPY, scale=gn_sb[:, t : t + 1])
 
-        last = PACK - 1
+        w2dw = late.tile([P, PACK, P], U32, name="w2dw", offset=0, align_bytes=64)
+        w2ds = late.tile([P, PACK, P], U8, name="w2ds", offset=2048, align_bytes=64)
+        deal(nc, w2dw[:].bitcast(I32), ww[:].bitcast(I32), every)
+        deal(nc, w2ds[:], ws[:], every)
+
         zw = keep.tile([P, S], U32, name="zw", align_bytes=64)
         zs = keep.tile([P, S], U8, name="zs", align_bytes=64)
         o32 = keep.tile([P, PACK, S], F32, name="o32", align_bytes=64)
@@ -141,8 +146,10 @@ def tile_picked_gossip2_none_po_kernel(
         osc = keep.tile([P, S], U8, name="osc", align_bytes=64)
         out_rows = out_0.rearrange("(p t) n -> p t n", t=PACK)
         chunks = [slice(c, c + CHUNK) for c in range(0, S, CHUNK)]
-        for c, cols in enumerate(chunks):
+        for cols in chunks:
             nc.scalar.activation(z[:, cols, last], h3[last][:, cols], COPY, scale=gn_sb[:, last : last + 1])
+        out_stores = {0: chunks[0], 2: slice(CHUNK, 3 * CHUNK), 3: chunks[3]}
+        word_stores = {2: slice(0, 3 * CHUNK), 3: chunks[3]}
         for c, cols in enumerate(chunks):
             nc.vector.quantize_mx(out=zw[:, cols].bitcast(FP8X4), scales=zs[:, cols], in_=z[:, cols, :].rearrange("p n t -> p (n t)"))
             acc = psum.tile([P, PACK, CHUNK], F32, name="bank%d" % (c + 1))
@@ -151,12 +158,21 @@ def tile_picked_gossip2_none_po_kernel(
                     out=acc[:, t, :], lhsT=w2dw[:, t, :].bitcast(FP8X4), lhsT_scale=w2ds[:, t, :],
                     rhs=zw[:, cols].bitcast(FP8X4), rhs_scale=zs[:, cols], start=True, stop=True,
                 )
+            if c == len(chunks) - 1:
+                nc.vector.tensor_copy(
+                    o16[:, cols, :].rearrange("p (c i) t -> p c t i", i=4), acc[:].rearrange("p t (c i) -> p c t i", i=4)
+                )
             nc.scalar.copy(o32[:, :, cols], acc[:])
-            nc.sync.dma_start(out=out_rows[:, :, cols], in_=o32[:, :, cols])
+            if c in out_stores:
+                nc.sync.dma_start(out=out_rows[:, :, out_stores[c]], in_=o32[:, :, out_stores[c]])
         for c, cols in enumerate(chunks):
-            nc.vector.tensor_copy(o16[:, cols, :], o32[:, :, cols].rearrange("p t n -> p n t"))
+            if c < len(chunks) - 1:
+                nc.vector.tensor_copy(
+                    o16[:, cols, :].rearrange("p (c i) t -> p c t i", i=4), o32[:, :, cols].rearrange("p t (c i) -> p c t i", i=4)
+                )
             nc.vector.quantize_mx(out=ow[:, cols].bitcast(FP8X4), scales=osc[:, cols], in_=o16[:, cols, :].rearrange("p n t -> p (n t)"))
-        nc.sync.dma_start(out=words_view(out_1), in_=ow[:].bitcast(I32))
+            if c in word_stores:
+                nc.sync.dma_start(out=words_view(out_1)[:, word_stores[c]], in_=ow[:, word_stores[c]].bitcast(I32))
         rows32 = out_2[0].bitcast(I32)
         for q in range(4):
             queue = nc.scalar if q % 2 else nc.sync

@@ -11,6 +11,7 @@ U8 = mybir.dt.uint8
 FP8X4 = mybir.dt.float8_e4m3fn_x4
 ALU = mybir.AluOpType
 COPY = mybir.ActivationFunctionType.Copy
+RELU = mybir.ActivationFunctionType.Relu
 
 P = 128
 PACK = 4
@@ -19,10 +20,10 @@ CHUNK = 128
 FLOPS = 2 * 2 * 512 * 512 * 512
 
 
-def load_scale_rows(queue, plane, rows):
+def load_scale_rows(queues, plane, rows):
     rows32 = rows.bitcast(I32)
     plane32 = plane[:].bitcast(I32)
-    for q in range(4):
+    for q, queue in enumerate(queues):
         queue.dma_start(out=plane32[32 * q : 32 * q + 4, :], in_=rows32[4 * q : 4 * q + 4, :])
 
 
@@ -61,14 +62,14 @@ def tile_picked_gossip2_none_po_kernel(
         ws = keep.tile([P, 512], U8, name="ws", align_bytes=64)
 
         nc.vector.memset(xs[:].bitcast(I32), 0)
-        nc.gpsimd.memset(ws[:].bitcast(I32), 0)
+        nc.vector.memset(ws[:].bitcast(I32), 0)
         nc.sync.dma_start(offs_sb[:], offs)
-        nc.sync.dma_start(la_sb[:], la)
-        nc.sync.dma_start(lb_sb[:], lb)
         nc.sync.dma_start(out=ww[:].bitcast(I32), in_=words_view(w1_words))
+        nc.sync.dma_start(la_sb[:], la)
+        load_scale_rows([nc.sync] * 4, xs, x_scales[0])
         nc.sync.dma_start(out=xw[:].bitcast(I32), in_=words_view(x_words))
-        load_scale_rows(nc.scalar, xs, x_scales[0])
-        load_scale_rows(nc.gpsimd, ws, w1_scales[0])
+        load_scale_rows([nc.sync] * 4, ws, w1_scales[0])
+        nc.sync.dma_start(lb_sb[:], lb)
         nc.sync.dma_start(ma_sb[:], ma)
         nc.sync.dma_start(mb_sb[:], mb)
 
@@ -87,7 +88,7 @@ def tile_picked_gossip2_none_po_kernel(
         gn_sb = keep.tile([P, PACK], F32, name="gn_sb", tag="xs", align_bytes=64)
         nc.sync.dma_start(out=gn_sb[:], in_=gn.rearrange("(p t) o -> p (t o)", t=PACK))
         nc.sync.dma_start(out=ww[:].bitcast(I32), in_=words_view(w2_words))
-        load_scale_rows(nc.sync, ws, w2_scales[0])
+        load_scale_rows([nc.sync] * 4, ws, w2_scales[0])
 
         yh = tiles("yh", [P, S], F32)
         pieces = [(0, cols) for cols in halves] + [(t, slice(0, S)) for t in range(1, PACK)]
@@ -99,39 +100,48 @@ def tile_picked_gossip2_none_po_kernel(
             )
             nc.scalar.activation(yh[t][:, cols], acc[:], COPY, scale=0.5)
 
-        ah = tiles("ah", [P, V], F32)
-        bh = tiles("bh", [P, V], F32)
-        pa = tiles("pa", [P, V], F32)
-        pb = tiles("pb", [P, V], F32)
+        def pair_tiles(name):
+            return tiles(name, [P, 2, V], F32, 2)
+
+        def of(pair, t):
+            return pair[t // 2][:, t % 2, :]
+
+        ah, bh, pa, pb = pair_tiles("ah"), pair_tiles("bh"), pair_tiles("pa"), pair_tiles("pb")
         h = tiles("h", [P, S], F32)
         for t in range(PACK):
-            nc.vector.tensor_copy(ah[t][:], yh[t][:].indirect(la_sb[:]))
-            nc.vector.tensor_copy(bh[t][:], yh[t][:].indirect(lb_sb[:]))
-            nc.scalar.activation(pa[t][:], ah[t][:], COPY, scale=-0.5)
-            nc.scalar.activation(pb[t][:], bh[t][:], COPY, scale=1.5)
+            nc.vector.tensor_copy(of(ah, t), yh[t][:].indirect(la_sb[:]))
+            nc.vector.tensor_copy(of(bh, t), yh[t][:].indirect(lb_sb[:]))
+        for u in range(2):
+            nc.scalar.activation(pa[u][:], ah[u][:], COPY, scale=-0.5)
+            nc.scalar.activation(pb[u][:], bh[u][:], COPY, scale=1.5)
         for t in range(PACK):
-            nc.vector.tensor_tensor(h[t][:].indirect(la_sb[:]), ah[t][:], bh[t][:], ALU.add)
+            nc.vector.tensor_tensor(h[t][:].indirect(lb_sb[:]), of(pa, t), of(pb, t), ALU.add)
         for t in range(PACK):
-            nc.vector.tensor_tensor(h[t][:].indirect(lb_sb[:]), pa[t][:], pb[t][:], ALU.add)
+            nc.vector.tensor_tensor(h[t][:].indirect(la_sb[:]), of(ah, t), of(bh, t), ALU.add)
 
-        ca = tiles("ca", [P, V], F32)
-        cb = tiles("cb", [P, V], F32)
-        hi = tiles("hi", [P, V], F32)
-        lo = tiles("lo", [P, V], F32, last) + [late.tile([P, V], F32, name="lo_last", offset=1536)]
+        hb, diff, up, under = pair_tiles("hb"), pair_tiles("diff"), pair_tiles("up"), pair_tiles("under")
+        down = tiles("down", [P, 2, V], F32, 1) + [late.tile([P, 2, V], F32, name="down_last", offset=1024)]
         h3 = tiles("h3_", [P, S], F32)
         for t in range(PACK):
-            nc.vector.tensor_copy(ca[t][:], h[t][:].indirect(ma_sb[:]))
-            nc.vector.tensor_copy(cb[t][:], h[t][:].indirect(mb_sb[:]))
+            nc.vector.tensor_copy(of(hb, t), h[t][:].indirect(mb_sb[:]))
         for t in range(PACK):
-            nc.vector.tensor_tensor(hi[t][:], ca[t][:], cb[t][:], ALU.max)
-            nc.vector.tensor_tensor(lo[t][:], ca[t][:], cb[t][:], ALU.min)
+            nc.vector.tensor_tensor(of(diff, t), h[t][:].indirect(ma_sb[:]), of(hb, t), ALU.subtract)
+        for u in range(2):
+            nc.scalar.activation(up[u][:], diff[u][:], RELU)
+        for u in range(2):
+            nc.scalar.activation(under[u][:], diff[u][:], RELU, scale=-1.0)
+            nc.scalar.activation(down[u][:], under[u][:], COPY, scale=-1.0)
         z = keep.tile([P, S, PACK], BF16, name="z", align_bytes=64)
+
+        def gain_and_round(t, cols):
+            nc.scalar.activation(z[:, cols, t], h3[t][:, cols], COPY, scale=gn_sb[:, t : t + 1])
+
         for t in range(PACK):
-            nc.vector.tensor_copy(h3[t][:].indirect(ma_sb[:]), hi[t][:])
+            nc.vector.tensor_tensor(h3[t][:].indirect(ma_sb[:]), of(hb, t), of(up, t), ALU.add)
         for t in range(PACK):
-            nc.vector.tensor_copy(h3[t][:].indirect(mb_sb[:]), lo[t][:])
+            nc.vector.tensor_tensor(h3[t][:].indirect(mb_sb[:]), of(hb, t), of(down, t), ALU.add)
             if t < last:
-                nc.scalar.activation(z[:, :, t], h3[t][:], COPY, scale=gn_sb[:, t : t + 1])
+                gain_and_round(t, slice(0, S if t < last - 1 else S - CHUNK))
 
         w2dw = late.tile([P, PACK, P], U32, name="w2dw", offset=0, align_bytes=64)
         w2ds = late.tile([P, PACK, P], U8, name="w2ds", offset=2048, align_bytes=64)
@@ -147,7 +157,9 @@ def tile_picked_gossip2_none_po_kernel(
         out_rows = out_0.rearrange("(p t) n -> p t n", t=PACK)
         chunks = [slice(c, c + CHUNK) for c in range(0, S, CHUNK)]
         for cols in chunks:
-            nc.scalar.activation(z[:, cols, last], h3[last][:, cols], COPY, scale=gn_sb[:, last : last + 1])
+            if cols == chunks[-1]:
+                gain_and_round(last - 1, cols)
+            gain_and_round(last, cols)
         out_stores = {0: chunks[0], 2: slice(CHUNK, 3 * CHUNK), 3: chunks[3]}
         word_stores = {2: slice(0, 3 * CHUNK), 3: chunks[3]}
         for c, cols in enumerate(chunks):

from contextlib import ExitStack

import concourse.mybir as mybir

F32 = mybir.dt.float32
BF16 = mybir.dt.bfloat16
I32 = mybir.dt.int32
U32 = mybir.dt.uint32
U16 = mybir.dt.uint16
U8 = mybir.dt.uint8
FP8X4 = mybir.dt.float8_e4m3fn_x4
ALU = mybir.AluOpType
COPY = mybir.ActivationFunctionType.Copy
RELU = mybir.ActivationFunctionType.Relu

P = 128
PACK = 4
T, S, V = 2048, 512, 256
CHUNK = 128
FLOPS = 2 * 2 * 512 * 512 * 512


def load_scale_rows(queues, plane, rows):
    rows32 = rows.bitcast(I32)
    plane32 = plane[:].bitcast(I32)
    for q, queue in enumerate(queues):
        queue.dma_start(out=plane32[32 * q : 32 * q + 4, :], in_=rows32[4 * q : 4 * q + 4, :])


def words_view(words):
    return words[0].rearrange("p n t -> p (n t)").bitcast(I32)


def deal(nc, dealt, raw, planes):
    nc.vector.tensor_copy(
        out=dealt.rearrange("p t m -> p m t")[:, :, planes], in_=raw.rearrange("p (m t) -> p m t", t=PACK)[:, :, planes]
    )


def tile_picked_gossip2_none_po_kernel(
    tc, x_words, x_scales, w1_words, w1_scales, gn, w2_words, w2_scales, offs, la, lb, ma, mb, out_0, out_1, out_2
):
    nc = tc.nc
    with ExitStack() as ctx:
        keep = ctx.enter_context(tc.tile_pool(name="keep", bufs=1))
        late = ctx.enter_context(tc.tile_pool(name="late", bufs=1))
        psum = ctx.enter_context(tc.psum_pool(name="psum", bufs=1))

        def tiles(name, shape, dtype, count=PACK):
            return [keep.tile(shape, dtype, name="%s%d" % (name, i), align_bytes=64) for i in range(count)]

        every = slice(0, PACK)
        last = PACK - 1
        offs_sb = keep.tile([P, S // 16], U16, name="offs_sb")
        la_sb = keep.tile([P, V // 16], U16, name="la_sb")
        lb_sb = keep.tile([P, V // 16], U16, name="lb_sb")
        ma_sb = keep.tile([P, V // 16], U16, name="ma_sb")
        mb_sb = keep.tile([P, V // 16], U16, name="mb_sb")
        xw = keep.tile([P, T], U32, name="xw", align_bytes=64)
        xs = keep.tile([P, T], U8, name="xs", tag="xs", align_bytes=64)
        ww = keep.tile([P, 512], U32, name="ww", align_bytes=64)
        ws = keep.tile([P, 512], U8, name="ws", align_bytes=64)

        nc.vector.memset(xs[:].bitcast(I32), 0)
        nc.vector.memset(ws[:].bitcast(I32), 0)
        nc.sync.dma_start(offs_sb[:], offs)
        nc.sync.dma_start(out=ww[:].bitcast(I32), in_=words_view(w1_words))
        nc.sync.dma_start(la_sb[:], la)
        load_scale_rows([nc.sync] * 4, xs, x_scales[0])
        nc.sync.dma_start(out=xw[:].bitcast(I32), in_=words_view(x_words))
        load_scale_rows([nc.sync] * 4, ws, w1_scales[0])
        nc.sync.dma_start(lb_sb[:], lb)
        nc.sync.dma_start(ma_sb[:], ma)
        nc.sync.dma_start(mb_sb[:], mb)

        w1dw = keep.tile([P, PACK, P], U32, name="w1dw", align_bytes=64)
        w1ds = keep.tile([P, PACK, P], U8, name="w1ds", align_bytes=64)
        deal(nc, w1dw[:].bitcast(I32), ww[:].bitcast(I32), every)
        xqw = keep.tile([P, S], U32, name="xqw", align_bytes=64)
        xqs = keep.tile([P, S], U8, name="xqs", align_bytes=64)
        nc.vector.tensor_copy(xqs[:], xs[:].indirect(offs_sb[:]))
        deal(nc, w1ds[:], ws[:], slice(0, 1))
        halves = [slice(0, S // 2), slice(S // 2, S)]
        for u, cols in enumerate(halves):
            nc.vector.tensor_copy(xqw[:, cols], xw[:].indirect(offs_sb[:, 16 * u : 16 * (u + 1)]))
        deal(nc, w1ds[:], ws[:], slice(1, PACK))

        gn_sb = keep.tile([P, PACK], F32, name="gn_sb", tag="xs", align_bytes=64)
        nc.sync.dma_start(out=gn_sb[:], in_=gn.rearrange("(p t) o -> p (t o)", t=PACK))
        nc.sync.dma_start(out=ww[:].bitcast(I32), in_=words_view(w2_words))
        load_scale_rows([nc.sync] * 4, ws, w2_scales[0])

        yh = tiles("yh", [P, S], F32)
        pieces = [(0, cols) for cols in halves] + [(t, slice(0, S)) for t in range(1, PACK)]
        for i, (t, cols) in enumerate(pieces):
            acc = psum.tile([P, cols.stop - cols.start], F32, name="bank%d" % i)
            nc.tensor.matmul_mx(
                out=acc[:], lhsT=w1dw[:, t, :].bitcast(FP8X4), lhsT_scale=w1ds[:, t, :],
                rhs=xqw[:, cols].bitcast(FP8X4), rhs_scale=xqs[:, cols], start=True, stop=True,
            )
            nc.scalar.activation(yh[t][:, cols], acc[:], COPY, scale=0.5)

        def pair_tiles(name):
            return tiles(name, [P, 2, V], F32, 2)

        def of(pair, t):
            return pair[t // 2][:, t % 2, :]

        ah, bh, pa, pb = pair_tiles("ah"), pair_tiles("bh"), pair_tiles("pa"), pair_tiles("pb")
        h = tiles("h", [P, S], F32)
        for t in range(PACK):
            nc.vector.tensor_copy(of(ah, t), yh[t][:].indirect(la_sb[:]))
            nc.vector.tensor_copy(of(bh, t), yh[t][:].indirect(lb_sb[:]))
        for u in range(2):
            nc.scalar.activation(pa[u][:], ah[u][:], COPY, scale=-0.5)
            nc.scalar.activation(pb[u][:], bh[u][:], COPY, scale=1.5)
        for t in range(PACK):
            nc.vector.tensor_tensor(h[t][:].indirect(lb_sb[:]), of(pa, t), of(pb, t), ALU.add)
        for t in range(PACK):
            nc.vector.tensor_tensor(h[t][:].indirect(la_sb[:]), of(ah, t), of(bh, t), ALU.add)

        hb, diff, up, under = pair_tiles("hb"), pair_tiles("diff"), pair_tiles("up"), pair_tiles("under")
        down = tiles("down", [P, 2, V], F32, 1) + [late.tile([P, 2, V], F32, name="down_last", offset=1024)]
        h3 = tiles("h3_", [P, S], F32)
        for t in range(PACK):
            nc.vector.tensor_copy(of(hb, t), h[t][:].indirect(mb_sb[:]))
        for t in range(PACK):
            nc.vector.tensor_tensor(of(diff, t), h[t][:].indirect(ma_sb[:]), of(hb, t), ALU.subtract)
        for u in range(2):
            nc.scalar.activation(up[u][:], diff[u][:], RELU)
        for u in range(2):
            nc.scalar.activation(under[u][:], diff[u][:], RELU, scale=-1.0)
            nc.scalar.activation(down[u][:], under[u][:], COPY, scale=-1.0)
        z = keep.tile([P, S, PACK], BF16, name="z", align_bytes=64)

        def gain_and_round(t, cols):
            nc.scalar.activation(z[:, cols, t], h3[t][:, cols], COPY, scale=gn_sb[:, t : t + 1])

        for t in range(PACK):
            nc.vector.tensor_tensor(h3[t][:].indirect(ma_sb[:]), of(hb, t), of(up, t), ALU.add)
        for t in range(PACK):
            nc.vector.tensor_tensor(h3[t][:].indirect(mb_sb[:]), of(hb, t), of(down, t), ALU.add)
            if t < last:
                gain_and_round(t, slice(0, S if t < last - 1 else S - CHUNK))

        w2dw = late.tile([P, PACK, P], U32, name="w2dw", offset=0, align_bytes=64)
        w2ds = late.tile([P, PACK, P], U8, name="w2ds", offset=2048, align_bytes=64)
        deal(nc, w2dw[:].bitcast(I32), ww[:].bitcast(I32), every)
        deal(nc, w2ds[:], ws[:], every)

        zw = keep.tile([P, S], U32, name="zw", align_bytes=64)
        zs = keep.tile([P, S], U8, name="zs", align_bytes=64)
        o32 = keep.tile([P, PACK, S], F32, name="o32", align_bytes=64)
        o16 = keep.tile([P, S, PACK], BF16, name="o16", align_bytes=64)
        ow = keep.tile([P, S], U32, name="ow", align_bytes=64)
        osc = keep.tile([P, S], U8, name="osc", align_bytes=64)
        out_rows = out_0.rearrange("(p t) n -> p t n", t=PACK)
        chunks = [slice(c, c + CHUNK) for c in range(0, S, CHUNK)]
        for cols in chunks:
            if cols == chunks[-1]:
                gain_and_round(last - 1, cols)
            gain_and_round(last, cols)
        out_stores = {0: chunks[0], 2: slice(CHUNK, 3 * CHUNK), 3: chunks[3]}
        word_stores = {2: slice(0, 3 * CHUNK), 3: chunks[3]}
        for c, cols in enumerate(chunks):
            nc.vector.quantize_mx(out=zw[:, cols].bitcast(FP8X4), scales=zs[:, cols], in_=z[:, cols, :].rearrange("p n t -> p (n t)"))
            acc = psum.tile([P, PACK, CHUNK], F32, name="bank%d" % (c + 1))
            for t in range(PACK):
                nc.tensor.matmul_mx(
                    out=acc[:, t, :], lhsT=w2dw[:, t, :].bitcast(FP8X4), lhsT_scale=w2ds[:, t, :],
                    rhs=zw[:, cols].bitcast(FP8X4), rhs_scale=zs[:, cols], start=True, stop=True,
                )
            if c == len(chunks) - 1:
                nc.vector.tensor_copy(
                    o16[:, cols, :].rearrange("p (c i) t -> p c t i", i=4), acc[:].rearrange("p t (c i) -> p c t i", i=4)
                )
            nc.scalar.copy(o32[:, :, cols], acc[:])
            if c in out_stores:
                nc.sync.dma_start(out=out_rows[:, :, out_stores[c]], in_=o32[:, :, out_stores[c]])
        for c, cols in enumerate(chunks):
            if c < len(chunks) - 1:
                nc.vector.tensor_copy(
                    o16[:, cols, :].rearrange("p (c i) t -> p c t i", i=4), o32[:, :, cols].rearrange("p t (c i) -> p c t i", i=4)
                )
            nc.vector.quantize_mx(out=ow[:, cols].bitcast(FP8X4), scales=osc[:, cols], in_=o16[:, cols, :].rearrange("p n t -> p (n t)"))
            if c in word_stores:
                nc.sync.dma_start(out=words_view(out_1)[:, word_stores[c]], in_=ow[:, word_stores[c]].bitcast(I32))
        rows32 = out_2[0].bitcast(I32)
        for q in range(4):
            queue = nc.scalar if q % 2 else nc.sync
            queue.dma_start(out=rows32[4 * q : 4 * q + 4, :], in_=osc[:].bitcast(I32)[32 * q : 32 * q + 4, :])
